import numpy as np, ml_dtypes
CORES = [1,14,19,24,37,42,55,60,65,78,83,88,101,106,119,124]
N = 16
TK = 128
def gelu(z): return 0.5 * z * (1.0 + np.tanh(0.7978845608028654 * (z + 0.044715 * z ** 3)))
def setup_inputs(rng):
    return {"x": rng.standard_normal((N, 128, TK), dtype=np.float32).astype(ml_dtypes.bfloat16), "w1": (rng.standard_normal((N, 128, 128), dtype=np.float32) / 8).astype(ml_dtypes.bfloat16), "w2": (rng.standard_normal((N, 128, 128), dtype=np.float32) / 8).astype(ml_dtypes.bfloat16)}
def setup_inputs_big(rng):
    d = setup_inputs(rng)
    for k in ("x",): d[k] = (d[k].astype(np.float32) * 1024.0).astype(d[k].dtype)
    return d
def setup_inputs_small(rng):
    d = setup_inputs(rng)
    for k in ("x",): d[k] = (d[k].astype(np.float32) * (1 / 1024.0)).astype(d[k].dtype)
    return d
def setup_inputs_apart(rng):
    d = setup_inputs(rng)
    f = (10.0 ** rng.permutation(np.linspace(-1.5, 1.5, N))).astype(np.float32).reshape(N, 1, 1)
    for k in ("x",): d[k] = (d[k].astype(np.float32) * f).astype(d[k].dtype)
    return d
def reference(x, w1, w2):
    X, W1, W2 = x.astype(np.float64), w1.astype(np.float64), w2.astype(np.float64)
    y = np.zeros((N, 128, TK))
    for r in range(N):
        for j in range(N):
            y[r] += W2[j].T @ (gelu(W1[j].T @ X[r]))
    return {"y": y.astype(ml_dtypes.bfloat16)}

@@ -1,0 +1,171 @@
+from concourse.bass import DstId, RemoteDMATransfer
+from concourse.mybir import ActivationFunctionType
+
+N = 16
+NH = 4
+DIRECT = 4
+PER = 2
+
+SCRATCH = {
+    "d": ("dram", [128, 256], "bfloat16"),
+    "wall": ("sbuf", [128, N * 256], "bfloat16"),
+    "xs": ("sbuf", [128, 128], "bfloat16"),
+    "hs": ("sbuf", [128, NH * 128], "bfloat16"),
+    "yo": ("sbuf", [128, 128], "bfloat16"),
+    "yp": ("psum", [128, 512], "float32"),
+}
+for _i in range(NH):
+    SCRATCH["hp%d" % _i] = ("psum", [128, 512], "float32")
+
+SEMAPHORES = (["ld_d", "ld_x", "ld_w", "hin", "loc", "ycp", "st"] + ["wa%d" % j for j in range(N)]
+              + ["m1_%d" % i for i in range(NH)] + ["ac_%d" % i for i in range(NH)] + ["m2_%d" % i for i in range(NH)])
+
+
+def _count(mask):
+    return bin(mask).count("1")
+
+
+def _by_die(cs, topo, last_die=None):
+    dies = sorted(set(topo.die(c) for c in cs), key=lambda x: (x == last_die, x))
+    groups = [[c for c in cs if topo.die(c) == x] for x in dies]
+    out = []
+    for i in range(max([len(q) for q in groups] + [0])):
+        for q in groups:
+            if i < len(q):
+                out.append(q[i])
+    return out
+
+
+def _plan(T, topo):
+    cores = list(T.cores)
+    chip = [topo.chip(c) for c in cores]
+    p0 = [r for r in range(N) if chip[r] == chip[0] or topo.same_plane(chip[r], chip[0])]
+    p1 = [[s for s in range(N) if topo.mates(chip[r], chip[s])][0] for r in p0]
+    every = range(topo.CHIPS * topo.CORES_PER_CHIP)
+    send, relay, when = {}, {}, {r: {r: -1.0} for r in range(N)}
+    load = {}
+
+    def give(ts, pool, got, cap):
+        for t in ts:
+            cs = [c for c in pool if len(got[c]) < cap[c]]
+            c = min(cs, key=lambda q: (load.get((chip[t], topo.die(q)), 0), pool.index(q)))
+            got[c].append(t)
+            load[(chip[t], topo.die(c))] = load.get((chip[t], topo.die(c)), 0) + 1
+
+    for own, oth in ((p0, p1), (p1, p0)):
+        n = len(own)
+        for i, k in enumerate(own):
+            me = cores[k]
+            cross = [oth[(i + s) % n] for s in range(n)]
+            plane = [own[(i + s) % n] for s in range(1, n)]
+            here = [c for c in every if topo.chip(c) == chip[k] and c != me]
+            can = _by_die([c for c in here if all(topo.may_write(c, cores[t]) for t in cross)], topo)
+            rest = _by_die([c for c in here if c not in can], topo, topo.die(me))
+            own_cross = max(0, len(cross) - PER * len(can))
+            rest = rest[:-(-(len(plane) - (DIRECT - own_cross)) // PER)]
+            got = {c: [] for c in [me] + can + rest}
+            cap = {c: PER for c in can + rest}
+            cap[me] = own_cross
+            give(cross, can + ([me] if own_cross else []), got, cap)
+            cap[me] = DIRECT
+            give(plane, [me] + rest, got, cap)
+            direct = got[me]
+            jobs = [(h, got[h]) for h in can + rest if got[h]]
+            send[k] = (direct, jobs)
+            for p, t in enumerate(direct):
+                when[t][k] = 1.0 + p
+            for hi, (h, ts) in enumerate(jobs):
+                relay[h] = (k, ts)
+                for p, t in enumerate(ts):
+                    when[t][k] = 4.0 + 0.2 * hi + p
+    order = {r: sorted(when[r], key=lambda s: (when[r][s], s)) for r in range(N)}
+    return send, relay, order
+
+
+def rank_program(g, core, T, topo):
+    send, relay, order = _plan(T, topo)
+    cores = list(T.cores)
+    S = T.sem
+    rank = T.rank_of(core)
+
+    def ids(cs):
+        return [DstId(rid=topo.addr(c)[0], pnc=topo.addr(c)[1]) for c in cs]
+
+    def mask_for(cs):
+        m = topo.mask(core, cs[0])
+        for c in cs[1:]:
+            m &= topo.mask(core, c)
+        return m
+
+    def slot(j, a=0, b=256):
+        return T.wall[:, j * 256 + a:j * 256 + b]
+
+    def to_ranks(k, ts):
+        cs = [cores[t] for t in ts]
+        m = mask_for(cs)
+        g.remote_dma_fused([RemoteDMATransfer(dst_ids=ids(cs), dma_engine_mask=m, remote_sem=S["wa%d" % k],
+                                              srcs=[T.d[:, :]], dsts=[slot(k) for _ in cs])], local_sem=S.loc)
+        return _count(m)
+
+    if rank is None:
+        if core not in relay:
+            return
+        k, ts = relay[core]
+        g.wait_ge(S.hin, _count(topo.mask(cores[k], core)))
+        g.wait_ge(S.loc, to_ranks(k, ts))
+        return
+
+    direct, jobs = send[rank]
+    g.sync.dma_start(T.d[:, 0:128], T.w1[:, :]).then_inc(S.ld_d, 16)
+    g.scalar.dma_start(T.d[:, 128:256], T.w2[:, :]).then_inc(S.ld_d, 16)
+    g.sync.dma_start(T.xs[:, :], T.x[:, :]).then_inc(S.ld_x, 16)
+    g.scalar.dma_start(slot(rank, 0, 128), T.w1[:, :]).then_inc(S.ld_w, 16)
+    g.sync.dma_start(slot(rank, 128, 256), T.w2[:, :]).then_inc(S.ld_w, 16)
+
+    g.wait_ge(S.ld_d, 32)
+    hs_ = [h for h, _ in jobs]
+    m_on = mask_for(hs_)
+    g.remote_dma_fused([RemoteDMATransfer(dst_ids=ids(hs_), dma_engine_mask=m_on, remote_sem=S.hin,
+                                          srcs=[T.d[:, :]], dsts=[T.d[:, :] for _ in hs_])], local_sem=S.loc)
+    left = _count(m_on) + to_ranks(rank, direct)
+
+    def landed(j):
+        dj, jj = send[j]
+        if rank in dj:
+            return _count(topo.mask(cores[j], core))
+        h = [h for h, ts in jj if rank in ts][0]
+        return _count(topo.mask(h, core))
+
+    te, ac, ve = g.tensor, g.scalar, g.vector
+    seq = order[rank]
+
+    def mm2(u):
+        s = u % NH
+        te.wait_ge(S["ac_%d" % s], u // NH + 1)
+        te.matmul(T.yp[:, 0:128], slot(seq[u], 128, 256), T.hs[:, s * 128:(s + 1) * 128],
+                  u == 0, u == N - 1).then_inc(S["m2_%d" % s], 1)
+
+    te.wait_ge(S.ld_x, 16)
+    for u, j in enumerate(seq):
+        s = u % NH
+        if j == rank:
+            te.wait_ge(S.ld_w, 32)
+        else:
+            te.wait_ge(S["wa%d" % j], landed(j))
+        te.matmul(T["hp%d" % s][:, 0:128], slot(j, 0, 128), T.xs[:, :], True, True).then_inc(S["m1_%d" % s], 1)
+        if u >= 1:
+            mm2(u - 1)
+        ac.wait_ge(S["m1_%d" % s], u // NH + 1)
+        if u >= NH:
+            ac.wait_ge(S["m2_%d" % s], u // NH)
+        ac.activation(T.hs[:, s * 128:(s + 1) * 128], T["hp%d" % s][:, 0:128],
+                      ActivationFunctionType.Gelu_apprx_tanh).then_inc(S["ac_%d" % s], 1)
+    mm2(N - 1)
+
+    for s in range(NH):
+        ve.wait_ge(S["m2_%d" % s], len([u for u in range(N) if u % NH == s]))
+    ve.tensor_copy(T.yo[:, :], T.yp[:, 0:128]).then_inc(S.ycp, 1)
+    g.sync.wait_ge(S.ycp, 1)
+    g.sync.dma_start(T.y[:, :], T.yo[:, :]).then_inc(S.st, 16)
+    g.sync.wait_ge(S.st, 16)
+    g.wait_ge(S.loc, left)

@@ -2,8 +2,9 @@ from concourse.bass import DstId, RemoteDMATransfer
 from concourse.mybir import ActivationFunctionType
 
 N = 16
-NH = 4
-DIRECT = 4
+NH = 6
+LAG = 3
+DIRECT = 5
 PER = 2
 
 SCRATCH = {
@@ -44,14 +45,13 @@ def _plan(T, topo):
     every = range(topo.CHIPS * topo.CORES_PER_CHIP)
     send, relay, when = {}, {}, {r: {r: -1.0} for r in range(N)}
     load = {}
+    early = {}
 
-    def give(ts, pool, got, cap):
-        for t in ts:
-            cs = [c for c in pool if len(got[c]) < cap[c]]
-            c = min(cs, key=lambda q: (load.get((chip[t], topo.die(q)), 0), pool.index(q)))
-            got[c].append(t)
-            load[(chip[t], topo.die(c))] = load.get((chip[t], topo.die(c)), 0) + 1
+    def add(t, c, p):
+        for key in ((chip[t], topo.die(c), p), (chip[t], topo.die(c))):
+            load[key] = load.get(key, 0) + 1
 
+    todo = []
     for own, oth in ((p0, p1), (p1, p0)):
         n = len(own)
         for i, k in enumerate(own):
@@ -61,23 +61,36 @@ def _plan(T, topo):
             here = [c for c in every if topo.chip(c) == chip[k] and c != me]
             can = _by_die([c for c in here if all(topo.may_write(c, cores[t]) for t in cross)], topo)
             rest = _by_die([c for c in here if c not in can], topo, topo.die(me))
-            own_cross = max(0, len(cross) - PER * len(can))
-            rest = rest[:-(-(len(plane) - (DIRECT - own_cross)) // PER)]
-            got = {c: [] for c in [me] + can + rest}
-            cap = {c: PER for c in can + rest}
-            cap[me] = own_cross
-            give(cross, can + ([me] if own_cross else []), got, cap)
-            cap[me] = DIRECT
-            give(plane, [me] + rest, got, cap)
-            direct = got[me]
-            jobs = [(h, got[h]) for h in can + rest if got[h]]
-            send[k] = (direct, jobs)
-            for p, t in enumerate(direct):
-                when[t][k] = 1.0 + p
-            for hi, (h, ts) in enumerate(jobs):
-                relay[h] = (k, ts)
-                for p, t in enumerate(ts):
-                    when[t][k] = 4.0 + 0.2 * hi + p
+            nc = min(len(cross), PER * len(can))
+            direct = cross[nc:]
+            take = max(0, DIRECT - len(direct))
+            direct = direct + plane[:take]
+            for t in direct:
+                add(t, me, "d")
+            todo.append((k, direct, [(cross[:nc], can), (plane[take:], rest)]))
+    for k, direct, parts in todo:
+        got = {}
+        for ts, pool in parts:
+            nh = -(-len(ts) // PER)
+            pool = pool[:nh]
+            ts = sorted(ts, key=lambda t: (early.get(t, 0), ts.index(t)))
+            for p in range(PER):
+                free = list(pool)
+                for t in ts[p * nh:(p + 1) * nh]:
+                    c = min(free, key=lambda q: (load.get((chip[t], topo.die(q), p), 0),
+                                                 load.get((chip[t], topo.die(q)), 0), pool.index(q)))
+                    free.remove(c)
+                    got.setdefault(c, []).append(t)
+                    add(t, c, p)
+                    early[t] = early.get(t, 0) + (1 if p == 0 else -1)
+        jobs = list(got.items())
+        send[k] = (direct, jobs)
+        for p, t in enumerate(direct):
+            when[t][k] = 1.95 + p
+        for hi, (h, ts) in enumerate(jobs):
+            relay[h] = (k, ts)
+            for p, t in enumerate(ts):
+                when[t][k] = 3.15 + 0.15 * hi + p
     order = {r: sorted(when[r], key=lambda s: (when[r][s], s)) for r in range(N)}
     return send, relay, order
 
@@ -91,10 +104,10 @@ def rank_program(g, core, T, topo):
     def ids(cs):
         return [DstId(rid=topo.addr(c)[0], pnc=topo.addr(c)[1]) for c in cs]
 
-    def mask_for(cs):
-        m = topo.mask(core, cs[0])
+    def mask_for(src, cs):
+        m = topo.mask(src, cs[0])
         for c in cs[1:]:
-            m &= topo.mask(core, c)
+            m &= topo.mask(src, c)
         return m
 
     def slot(j, a=0, b=256):
@@ -102,7 +115,7 @@ def rank_program(g, core, T, topo):
 
     def to_ranks(k, ts):
         cs = [cores[t] for t in ts]
-        m = mask_for(cs)
+        m = mask_for(core, cs)
         g.remote_dma_fused([RemoteDMATransfer(dst_ids=ids(cs), dma_engine_mask=m, remote_sem=S["wa%d" % k],
                                               srcs=[T.d[:, :]], dsts=[slot(k) for _ in cs])], local_sem=S.loc)
         return _count(m)
@@ -111,7 +124,7 @@ def rank_program(g, core, T, topo):
         if core not in relay:
             return
         k, ts = relay[core]
-        g.wait_ge(S.hin, _count(topo.mask(cores[k], core)))
+        g.wait_ge(S.hin, _count(mask_for(cores[k], [h for h, _ in send[k][1]])))
         g.wait_ge(S.loc, to_ranks(k, ts))
         return
 
@@ -124,7 +137,7 @@ def rank_program(g, core, T, topo):
 
     g.wait_ge(S.ld_d, 32)
     hs_ = [h for h, _ in jobs]
-    m_on = mask_for(hs_)
+    m_on = mask_for(core, hs_)
     g.remote_dma_fused([RemoteDMATransfer(dst_ids=ids(hs_), dma_engine_mask=m_on, remote_sem=S.hin,
                                           srcs=[T.d[:, :]], dsts=[T.d[:, :] for _ in hs_])], local_sem=S.loc)
     left = _count(m_on) + to_ranks(rank, direct)
@@ -132,9 +145,9 @@ def rank_program(g, core, T, topo):
     def landed(j):
         dj, jj = send[j]
         if rank in dj:
-            return _count(topo.mask(cores[j], core))
-        h = [h for h, ts in jj if rank in ts][0]
-        return _count(topo.mask(h, core))
+            return _count(mask_for(cores[j], [cores[t] for t in dj]))
+        h, ts = [(h, ts) for h, ts in jj if rank in ts][0]
+        return _count(mask_for(h, [cores[t] for t in ts]))
 
     te, ac, ve = g.tensor, g.scalar, g.vector
     seq = order[rank]
@@ -153,14 +166,15 @@ def rank_program(g, core, T, topo):
         else:
             te.wait_ge(S["wa%d" % j], landed(j))
         te.matmul(T["hp%d" % s][:, 0:128], slot(j, 0, 128), T.xs[:, :], True, True).then_inc(S["m1_%d" % s], 1)
-        if u >= 1:
-            mm2(u - 1)
+        if u >= LAG:
+            mm2(u - LAG)
         ac.wait_ge(S["m1_%d" % s], u // NH + 1)
         if u >= NH:
             ac.wait_ge(S["m2_%d" % s], u // NH)
         ac.activation(T.hs[:, s * 128:(s + 1) * 128], T["hp%d" % s][:, 0:128],
                       ActivationFunctionType.Gelu_apprx_tanh).then_inc(S["ac_%d" % s], 1)
-    mm2(N - 1)
+    for u in range(N - LAG, N):
+        mm2(u)
 
     for s in range(NH):
         ve.wait_ge(S["m2_%d" % s], len([u for u in range(N) if u % NH == s]))

from concourse.bass import DstId, RemoteDMATransfer
from concourse.mybir import ActivationFunctionType

N = 16
NH = 6
LAG = 3
DIRECT = 5
PER = 2

SCRATCH = {
    "d": ("dram", [128, 256], "bfloat16"),
    "wall": ("sbuf", [128, N * 256], "bfloat16"),
    "xs": ("sbuf", [128, 128], "bfloat16"),
    "hs": ("sbuf", [128, NH * 128], "bfloat16"),
    "yo": ("sbuf", [128, 128], "bfloat16"),
    "yp": ("psum", [128, 512], "float32"),
}
for _i in range(NH):
    SCRATCH["hp%d" % _i] = ("psum", [128, 512], "float32")

SEMAPHORES = (["ld_d", "ld_x", "ld_w", "hin", "loc", "ycp", "st"] + ["wa%d" % j for j in range(N)]
              + ["m1_%d" % i for i in range(NH)] + ["ac_%d" % i for i in range(NH)] + ["m2_%d" % i for i in range(NH)])


def _count(mask):
    return bin(mask).count("1")


def _by_die(cs, topo, last_die=None):
    dies = sorted(set(topo.die(c) for c in cs), key=lambda x: (x == last_die, x))
    groups = [[c for c in cs if topo.die(c) == x] for x in dies]
    out = []
    for i in range(max([len(q) for q in groups] + [0])):
        for q in groups:
            if i < len(q):
                out.append(q[i])
    return out


def _plan(T, topo):
    cores = list(T.cores)
    chip = [topo.chip(c) for c in cores]
    p0 = [r for r in range(N) if chip[r] == chip[0] or topo.same_plane(chip[r], chip[0])]
    p1 = [[s for s in range(N) if topo.mates(chip[r], chip[s])][0] for r in p0]
    every = range(topo.CHIPS * topo.CORES_PER_CHIP)
    send, relay, when = {}, {}, {r: {r: -1.0} for r in range(N)}
    load = {}
    early = {}

    def add(t, c, p):
        for key in ((chip[t], topo.die(c), p), (chip[t], topo.die(c))):
            load[key] = load.get(key, 0) + 1

    todo = []
    for own, oth in ((p0, p1), (p1, p0)):
        n = len(own)
        for i, k in enumerate(own):
            me = cores[k]
            cross = [oth[(i + s) % n] for s in range(n)]
            plane = [own[(i + s) % n] for s in range(1, n)]
            here = [c for c in every if topo.chip(c) == chip[k] and c != me]
            can = _by_die([c for c in here if all(topo.may_write(c, cores[t]) for t in cross)], topo)
            rest = _by_die([c for c in here if c not in can], topo, topo.die(me))
            nc = min(len(cross), PER * len(can))
            direct = cross[nc:]
            take = max(0, DIRECT - len(direct))
            direct = direct + plane[:take]
            for t in direct:
                add(t, me, "d")
            todo.append((k, direct, [(cross[:nc], can), (plane[take:], rest)]))
    for k, direct, parts in todo:
        got = {}
        for ts, pool in parts:
            nh = -(-len(ts) // PER)
            pool = pool[:nh]
            ts = sorted(ts, key=lambda t: (early.get(t, 0), ts.index(t)))
            for p in range(PER):
                free = list(pool)
                for t in ts[p * nh:(p + 1) * nh]:
                    c = min(free, key=lambda q: (load.get((chip[t], topo.die(q), p), 0),
                                                 load.get((chip[t], topo.die(q)), 0), pool.index(q)))
                    free.remove(c)
                    got.setdefault(c, []).append(t)
                    add(t, c, p)
                    early[t] = early.get(t, 0) + (1 if p == 0 else -1)
        jobs = list(got.items())
        send[k] = (direct, jobs)
        for p, t in enumerate(direct):
            when[t][k] = 1.95 + p
        for hi, (h, ts) in enumerate(jobs):
            relay[h] = (k, ts)
            for p, t in enumerate(ts):
                when[t][k] = 3.15 + 0.15 * hi + p
    order = {r: sorted(when[r], key=lambda s: (when[r][s], s)) for r in range(N)}
    return send, relay, order


def rank_program(g, core, T, topo):
    send, relay, order = _plan(T, topo)
    cores = list(T.cores)
    S = T.sem
    rank = T.rank_of(core)

    def ids(cs):
        return [DstId(rid=topo.addr(c)[0], pnc=topo.addr(c)[1]) for c in cs]

    def mask_for(src, cs):
        m = topo.mask(src, cs[0])
        for c in cs[1:]:
            m &= topo.mask(src, c)
        return m

    def slot(j, a=0, b=256):
        return T.wall[:, j * 256 + a:j * 256 + b]

    def to_ranks(k, ts):
        cs = [cores[t] for t in ts]
        m = mask_for(core, cs)
        g.remote_dma_fused([RemoteDMATransfer(dst_ids=ids(cs), dma_engine_mask=m, remote_sem=S["wa%d" % k],
                                              srcs=[T.d[:, :]], dsts=[slot(k) for _ in cs])], local_sem=S.loc)
        return _count(m)

    if rank is None:
        if core not in relay:
            return
        k, ts = relay[core]
        g.wait_ge(S.hin, _count(mask_for(cores[k], [h for h, _ in send[k][1]])))
        g.wait_ge(S.loc, to_ranks(k, ts))
        return

    direct, jobs = send[rank]
    g.sync.dma_start(T.d[:, 0:128], T.w1[:, :]).then_inc(S.ld_d, 16)
    g.scalar.dma_start(T.d[:, 128:256], T.w2[:, :]).then_inc(S.ld_d, 16)
    g.sync.dma_start(T.xs[:, :], T.x[:, :]).then_inc(S.ld_x, 16)
    g.scalar.dma_start(slot(rank, 0, 128), T.w1[:, :]).then_inc(S.ld_w, 16)
    g.sync.dma_start(slot(rank, 128, 256), T.w2[:, :]).then_inc(S.ld_w, 16)

    g.wait_ge(S.ld_d, 32)
    hs_ = [h for h, _ in jobs]
    m_on = mask_for(core, hs_)
    g.remote_dma_fused([RemoteDMATransfer(dst_ids=ids(hs_), dma_engine_mask=m_on, remote_sem=S.hin,
                                          srcs=[T.d[:, :]], dsts=[T.d[:, :] for _ in hs_])], local_sem=S.loc)
    left = _count(m_on) + to_ranks(rank, direct)

    def landed(j):
        dj, jj = send[j]
        if rank in dj:
            return _count(mask_for(cores[j], [cores[t] for t in dj]))
        h, ts = [(h, ts) for h, ts in jj if rank in ts][0]
        return _count(mask_for(h, [cores[t] for t in ts]))

    te, ac, ve = g.tensor, g.scalar, g.vector
    seq = order[rank]

    def mm2(u):
        s = u % NH
        te.wait_ge(S["ac_%d" % s], u // NH + 1)
        te.matmul(T.yp[:, 0:128], slot(seq[u], 128, 256), T.hs[:, s * 128:(s + 1) * 128],
                  u == 0, u == N - 1).then_inc(S["m2_%d" % s], 1)

    te.wait_ge(S.ld_x, 16)
    for u, j in enumerate(seq):
        s = u % NH
        if j == rank:
            te.wait_ge(S.ld_w, 32)
        else:
            te.wait_ge(S["wa%d" % j], landed(j))
        te.matmul(T["hp%d" % s][:, 0:128], slot(j, 0, 128), T.xs[:, :], True, True).then_inc(S["m1_%d" % s], 1)
        if u >= LAG:
            mm2(u - LAG)
        ac.wait_ge(S["m1_%d" % s], u // NH + 1)
        if u >= NH:
            ac.wait_ge(S["m2_%d" % s], u // NH)
        ac.activation(T.hs[:, s * 128:(s + 1) * 128], T["hp%d" % s][:, 0:128],
                      ActivationFunctionType.Gelu_apprx_tanh).then_inc(S["ac_%d" % s], 1)
    for u in range(N - LAG, N):
        mm2(u)

    for s in range(NH):
        ve.wait_ge(S["m2_%d" % s], len([u for u in range(N) if u % NH == s]))
    ve.tensor_copy(T.yo[:, :], T.yp[:, 0:128]).then_inc(S.ycp, 1)
    g.sync.wait_ge(S.ycp, 1)
    g.sync.dma_start(T.y[:, :], T.yo[:, :]).then_inc(S.st, 16)
    g.sync.wait_ge(S.st, 16)
    g.wait_ge(S.loc, left)
